import numpy as np
import ml_dtypes


def mxq(x, axis, fmt="e4m3"):
    dtype, down = {"e4m3": (ml_dtypes.float8_e4m3fn, 7), "e5m2": (ml_dtypes.float8_e5m2, 14)}[fmt]
    v = np.moveaxis(np.asarray(x, np.float32).astype(ml_dtypes.bfloat16).astype(np.float64), axis, -1)
    blocks = v.reshape(v.shape[:-1] + (-1, 32))
    amax = np.abs(blocks).max(-1, keepdims=True)
    byte = np.maximum(np.where(amax > 0, np.frexp(amax)[1] - 1 + 127, 0) - down, 1)
    scale = np.exp2(byte - 127.0)
    codes = (blocks / scale).astype(np.float32).astype(dtype).astype(np.float64)
    return np.moveaxis((codes * scale).reshape(v.shape), -1, axis)


WIDE = False


def mx_kscale(k):
    if not WIDE:
        return np.ones(k)
    levels = np.array([10, -10, 5, -5, 0])
    if k % 512:
        return np.exp2(np.random.permutation(np.resize(levels, k // 32))).repeat(32)
    a = np.empty((k // 512, 16))
    for p in range(k // 512):
        a[p, :8] = np.random.permutation(np.resize(levels, 8))
        for g in range(8):
            far = levels[np.abs(levels - a[p, g]) >= 10]
            a[p, g + 8] = far[np.random.randint(len(far))]
    return np.exp2(a.ravel()).repeat(32)


def f64(x):
    return np.asarray(x).astype(np.float64)


def striped(idx):
    return np.tile(idx.reshape(-1, 16).T, (8, 1)).astype(np.uint16)


def unstriped(offs):
    return offs[:16].T.reshape(-1).astype(np.int64)


E2M1 = np.array([0.0, 0.5, 1.0, 1.5, 2.0, 3.0, 4.0, 6.0, -0.0, -0.5, -1.0, -1.5, -2.0, -3.0, -4.0, -6.0])


def pack_weight(w, fmt):
    k, n = w.shape
    w = f64(np.asarray(w, np.float32).astype(ml_dtypes.bfloat16)).reshape(k // 32, 32, n)
    amax = np.abs(w).max(1)
    if fmt == "e4m3":
        byte = np.frexp(amax)[1] - 1 + 127 - 7
    else:
        mant, ex = np.frexp(amax / 6.0)
        byte = np.where(mant > 0.5, ex, ex - 1) + 127
    byte = np.clip(np.where(amax > 0, byte, 1), 1, 254)
    scaled = (w * np.exp2(127.0 - byte)[:, None, :]).reshape(k, n).astype(np.float32)
    by_word = np.ascontiguousarray(scaled.reshape(k // 512, 128, 4, n).transpose(0, 1, 3, 2))
    if fmt == "e4m3":
        words = by_word.astype(ml_dtypes.float8_e4m3fn).view(np.uint8)
    else:
        c = by_word.astype(ml_dtypes.float4_e2m1fn).view(np.uint8) & 0xF
        words = (c[..., 0::2] | (c[..., 1::2] << 4)).reshape(k // 512, 128, 2 * n)
    return np.ascontiguousarray(words), np.ascontiguousarray(byte.astype(np.uint8).reshape(k // 512, 16, n))


def unpack_weight(words, scales, fmt):
    g, _, n = scales.shape
    words = np.ascontiguousarray(words).reshape(g, 128, n, -1)
    if fmt == "e4m3":
        vals = words.view(ml_dtypes.float8_e4m3fn).astype(np.float64)
    else:
        nib = np.empty((g, 128, n, 4), np.uint8)
        nib[..., 0::2] = words & 0xF
        nib[..., 1::2] = words >> 4
        vals = E2M1[nib]
    vals = vals * np.repeat(np.exp2(scales.astype(np.float64) - 127.0), 8, axis=1)[..., None]
    return vals.transpose(0, 1, 3, 2).reshape(g * 512, n)


def relu(v):
    return np.maximum(v, 0.0)


K, T, E, C, N = 1536, 512, 8, 128, 512
M = 384


def by_expert(wq, xq):
    return np.concatenate([wq[e].T @ xq[:, e * C:(e + 1) * C] for e in range(E)], axis=1)


def setup_inputs():
    n = np.random.standard_normal
    s = mx_kscale(K)[:, None]
    v = mx_kscale(N)
    first = np.random.permutation(np.repeat(np.arange(E), T // E))
    second = (first + 1 + np.random.permutation(np.repeat(np.arange(E - 1), -(-T // (E - 1)))[:T])) % E
    while np.bincount(second, minlength=E).max() != T // E:
        load = np.bincount(second, minlength=E); hi, lo = int(load.argmax()), int(load.argmin())
        t = np.flatnonzero((second == hi) & (first != lo))[0]; second[t] = lo
    slot_token = np.empty(E * C, np.int64); pos = np.empty((2, T), np.int64); fill = np.zeros(E, np.int64)
    place = np.stack([np.random.permutation(C) for _ in range(E)])
    for r, deal in enumerate((first, second)):
        for t in np.random.permutation(T):
            e = deal[t]; j = e * C + place[e, fill[e]]; fill[e] += 1; slot_token[j] = t; pos[r, t] = j
    g = np.random.uniform(0.2, 0.8, T)
    w = [pack_weight(m, "e2m1") for m in n((E, K, N)) / np.sqrt(K) / s[None] * v[None, None, :]]
    return {
        "xT": (n((K, T)) * s).astype(np.float32),
        "w_words": np.stack([m[0] for m in w]),
        "w_scales": np.stack([m[1] for m in w]),
        "b": (0.3 * n((N, E)) * v[:, None]).astype(np.float32),
        "wp": (n((N, M)) / np.sqrt(N) / v[:, None]).astype(np.float32),
        "gate": np.stack([np.tile(g, (N, 1)), np.tile(1.0 - g, (N, 1))]).astype(np.float32),
        "offs": striped(slot_token),
        "pos1": striped(pos[0]),
        "pos2": striped(pos[1]),
    }


def reference(xT, w_words, w_scales, b, wp, gate, offs, pos1, pos2):
    idx = unstriped(offs)
    w = np.stack([unpack_weight(w_words[e], w_scales[e], "e2m1") for e in range(E)])
    xq = mxq(f64(xT)[:, idx], 0, "e4m3")
    y = by_expert(w, xq)
    y = relu(y + np.repeat(f64(b), C, axis=1))
    c = f64(gate[0]) * y[:, unstriped(pos1)] + f64(gate[1]) * y[:, unstriped(pos2)]
    return mxq(f64(wp), 0, "e4m3").T @ mxq(c, 0, "e4m3")

@@ -1,0 +1,176 @@
+from contextlib import ExitStack
+
+import concourse.mybir as mybir
+from concourse.masks import make_identity
+
+K, T, E, C, N, M = 1536, 512, 8, 128, 512, 384
+P = 128
+A = 3
+R = 4
+HALF = 256
+CHUNKS = ((0, 3), (3, 6), (6, 8))
+FLOPS = 2 * K * N * E * C + 2 * N * M * T
+BYTES = 4 * K * T + E * K * N // 2 + E * K * N // 32 + 4 * N * E + 4 * N * M + 4 * 2 * T + 2 * 128 * 128 + 4 * M * T
+
+F32 = mybir.dt.float32
+BF16 = mybir.dt.bfloat16
+I32 = mybir.dt.int32
+U32 = mybir.dt.uint32
+U16 = mybir.dt.uint16
+U8 = mybir.dt.uint8
+FP8X4 = mybir.dt.float8_e4m3fn_x4
+FP4X4 = mybir.dt.float4_e2m1fn_x4
+ACT = mybir.ActivationFunctionType
+ALU = mybir.AluOpType
+
+
+def tile_moe_nxt_lin_relu_kernel(tc, xT, w_words, w_scales, b, wp, gate, offs, pos1, pos2, out):
+    nc = tc.nc
+    with ExitStack() as ctx:
+        keep = ctx.enter_context(tc.tile_pool(name="keep", bufs=1))
+        ring = ctx.enter_context(tc.tile_pool(name="ring", bufs=3))
+        acc_pool = ctx.enter_context(tc.psum_pool(name="acc_pool", bufs=4))
+        turn_pool = ctx.enter_context(tc.psum_pool(name="turn_pool", bufs=4))
+
+        offs_t = keep.tile([P, E * C // 16], U16, name="offs_t")
+        pos1_t = keep.tile([P, T // 16], U16, name="pos1_t")
+        pos2_t = keep.tile([P, T // 16], U16, name="pos2_t")
+        x_raw = [[keep.tile([P, 4, HALF], F32, name=f"x_raw{a}_{h}") for h in range(2)] for a in range(A)]
+        w_t = [keep.tile([P, A, 2 * N], U8, name=f"w_t{e}", align_bytes=64) for e in range(E)]
+        ws_t = keep.tile([P, E * A, N], U8, name="ws_t", align_bytes=64)
+        b_t = keep.tile([P, R, E], F32, name="b_t")
+        gate_t = keep.tile([P, 2, T], F32, name="gate_t")
+        wp_raw = keep.tile([P, 4, M], F32, name="wp_raw")
+
+        nc.vector.memset(ws_t[:].rearrange("p g n -> p (g n)").bitcast(I32), 0)
+
+        nc.sync.dma_start(offs_t[:], offs)
+        for a in range(A):
+            rows = xT[512 * a : 512 * (a + 1), :].rearrange("(p j) t -> p j t", j=4)
+            for h in range(2):
+                nc.sync.dma_start(out=x_raw[a][h][:], in_=rows[:, :, h * HALF : (h + 1) * HALF])
+        scale_rows = w_scales.rearrange("e a q n -> q (e a) n")
+        for i in range(4):
+            nc.sync.dma_start(out=ws_t[i:P:32, :, :].bitcast(I32), in_=scale_rows[i:16:4, :, :].bitcast(I32))
+        for e in range(E):
+            nc.sync.dma_start(out=w_t[e][:].bitcast(I32), in_=w_words[e].rearrange("a p c -> p a c").bitcast(I32))
+            if e == 0:
+                nc.sync.dma_start(out=b_t[:], in_=b.rearrange("(p r) e -> p r e", r=R))
+        nc.sync.dma_start(pos1_t[:], pos1)
+        nc.sync.dma_start(pos2_t[:], pos2)
+        nc.sync.dma_start(out=gate_t[:], in_=gate[:, 0:P, :].rearrange("g p t -> p g t"))
+        nc.sync.dma_start(out=wp_raw[:], in_=wp.rearrange("(p j) f -> p j f", j=4))
+
+        ident = keep.tile([P, P], F32, name="ident")
+        make_identity(nc, ident[:])
+
+        codes = [keep.tile([P, T], U32, name=f"codes{a}", align_bytes=64) for a in range(A)]
+        planes = [keep.tile([P, T], U8, name=f"planes{a}", align_bytes=64) for a in range(A)]
+        slot_codes = [keep.tile([P, E * C], U32, name=f"slot_codes{a}", align_bytes=64) for a in range(A)]
+        slot_planes = [keep.tile([P, E * C], U8, name=f"slot_planes{a}", align_bytes=64) for a in range(A)]
+        for a in range(A):
+            nc.gpsimd.memset(planes[a][:].bitcast(I32), 0)
+
+        def quantise_pass(a):
+            for h in range(2):
+                cols = slice(h * HALF, (h + 1) * HALF)
+                x_b = keep.tile([P, HALF, 4], BF16, name=f"x_b{a}_{h}", align_bytes=64)
+                dst = x_b[:].rearrange("p (c i) j -> p c j i", i=4)
+                src = x_raw[a][h][:].rearrange("p j (c i) -> p c j i", i=4)
+                if h == 0 and a != 1:
+                    nc.vector.tensor_copy(out=dst, in_=src)
+                else:
+                    nc.scalar.activation(out=dst, in_=src, func=ACT.Copy)
+                nc.vector.quantize_mx(
+                    out=codes[a][:, cols].bitcast(FP8X4), scales=planes[a][:, cols], in_=x_b[:].rearrange("p c j -> p (c j)")
+                )
+
+        def gather(a, chunk):
+            e0, e1 = chunk
+            slots = slice(e0 * C, e1 * C)
+            offsets = offs_t[:, e0 * C // 16 : e1 * C // 16]
+            nc.vector.tensor_copy(out=slot_codes[a][:, slots], in_=codes[a][:].indirect(offsets))
+            nc.vector.tensor_copy(out=slot_planes[a][:, slots], in_=planes[a][:].indirect(offsets))
+
+        y = [keep.tile([P, E * C], F32, name=f"y{r}") for r in range(R)]
+
+        def expert(e):
+            slots = slice(e * C, (e + 1) * C)
+            acc = acc_pool.tile([P, N], F32)
+            for a in range(A):
+                nc.tensor.matmul_mx(
+                    out=acc[:],
+                    lhsT=slot_codes[a][:, slots].bitcast(FP8X4),
+                    lhsT_scale=slot_planes[a][:, slots],
+                    rhs=w_t[e][:, a, :].bitcast(FP4X4),
+                    rhs_scale=ws_t[:, e * A + a, :],
+                    start=(a == 0),
+                    stop=(a == A - 1),
+                )
+            z = ring.tile([P, R, P], F32)
+            nc.scalar.activation(out=z[:], in_=acc[:].rearrange("s (m r) -> s r m", r=R), func=ACT.Copy)
+            turned = turn_pool.tile([P, R, C], F32)
+            for r in range(R):
+                nc.tensor.transpose(turned[:, r, :], z[:, r, :], ident[:])
+            for r in range(R):
+                nc.scalar.activation(out=y[r][:, slots], in_=turned[:, r, :], func=ACT.Relu, bias=b_t[:, r, e : e + 1], scale=1.0)
+
+        for a in range(A - 1):
+            quantise_pass(a)
+            for chunk in CHUNKS:
+                gather(a, chunk)
+        quantise_pass(A - 1)
+        for chunk in CHUNKS:
+            gather(A - 1, chunk)
+            for e in range(chunk[0], chunk[1]):
+                expert(e)
+
+        wp_b = keep.tile([P, M, 4], BF16, name="wp_b", align_bytes=64)
+        nc.scalar.activation(
+            out=wp_b[:].rearrange("p (c i) j -> p c j i", i=4), in_=wp_raw[:].rearrange("p j (c i) -> p c j i", i=4), func=ACT.Copy
+        )
+        wp_codes = keep.tile([P, M], U32, name="wp_codes", align_bytes=64)
+        wp_planes = keep.tile([P, M], U8, name="wp_planes", align_bytes=64)
+        for lo, hi in ((0, 256), (256, 384)):
+            nc.vector.quantize_mx(
+                out=wp_codes[:, lo:hi].bitcast(FP8X4), scales=wp_planes[:, lo:hi], in_=wp_b[:, lo:hi, :].rearrange("p c j -> p (c j)")
+            )
+
+        out_rows = out.rearrange("(f p) t -> p f t", p=P)
+        for h in range(2):
+            toks = slice(h * HALF, (h + 1) * HALF)
+            idx = slice(h * HALF // 16, (h + 1) * HALF // 16)
+            g1 = keep.tile([P, R, HALF], F32, name=f"g1_{h}")
+            g2 = keep.tile([P, R, HALF], F32, name=f"g2_{h}")
+            for r in range(R):
+                nc.vector.tensor_tensor(g1[:, r, :], y[r][:].indirect(pos1_t[:, idx]), gate_t[:, 0, toks], ALU.mult)
+                nc.vector.tensor_tensor(g2[:, r, :], y[r][:].indirect(pos2_t[:, idx]), gate_t[:, 1, toks], ALU.mult)
+            c_b = keep.tile([P, HALF, R], BF16, name=f"c_b{h}", align_bytes=64)
+            nc.vector.tensor_tensor(
+                c_b[:].rearrange("p (c i) r -> p c r i", i=4),
+                g1[:].rearrange("p r (c i) -> p c r i", i=4),
+                g2[:].rearrange("p r (c i) -> p c r i", i=4),
+                ALU.add,
+            )
+            c_codes = keep.tile([P, HALF], U32, name=f"c_codes{h}", align_bytes=64)
+            c_planes = keep.tile([P, HALF], U8, name=f"c_planes{h}", align_bytes=64)
+            nc.vector.quantize_mx(out=c_codes[:].bitcast(FP8X4), scales=c_planes[:], in_=c_b[:].rearrange("p c r -> p (c r)"))
+            result = keep.tile([P, 3, HALF], F32, name=f"result{h}")
+            for f0, f1 in ((0, 2), (2, 3)):
+                acc = acc_pool.tile([P, N], F32)
+                for f in range(f0, f1):
+                    nc.tensor.matmul_mx(
+                        out=acc[:, (f - f0) * HALF : (f - f0 + 1) * HALF],
+                        lhsT=wp_codes[:, f * P : (f + 1) * P].bitcast(FP8X4),
+                        lhsT_scale=wp_planes[:, f * P : (f + 1) * P],
+                        rhs=c_codes[:].bitcast(FP8X4),
+                        rhs_scale=c_planes[:],
+                        start=True,
+                        stop=True,
+                    )
+                sums = acc[:, 0 : (f1 - f0) * HALF].rearrange("p (f t) -> p f t", t=HALF)
+                if h == 1 and f0 == 2:
+                    nc.vector.tensor_copy(out=result[:, f0:f1, :], in_=sums)
+                else:
+                    nc.scalar.activation(out=result[:, f0:f1, :], in_=sums, func=ACT.Copy)
+                nc.sync.dma_start(out=out_rows[:, f0:f1, toks], in_=result[:, f0:f1, :])

@@ -8,7 +8,7 @@ P = 128
 A = 3
 R = 4
 HALF = 256
-CHUNKS = ((0, 3), (3, 6), (6, 8))
+WINDOW = 1376
 FLOPS = 2 * K * N * E * C + 2 * N * M * T
 BYTES = 4 * K * T + E * K * N // 2 + E * K * N // 32 + 4 * N * E + 4 * N * M + 4 * 2 * T + 2 * 128 * 128 + 4 * M * T
 
@@ -28,6 +28,7 @@ def tile_moe_nxt_lin_relu_kernel(tc, xT, w_words, w_scales, b, wp, gate, offs, p
     nc = tc.nc
     with ExitStack() as ctx:
         keep = ctx.enter_context(tc.tile_pool(name="keep", bufs=1))
+        late = ctx.enter_context(tc.tile_pool(name="late", bufs=1))
         ring = ctx.enter_context(tc.tile_pool(name="ring", bufs=3))
         acc_pool = ctx.enter_context(tc.psum_pool(name="acc_pool", bufs=4))
         turn_pool = ctx.enter_context(tc.psum_pool(name="turn_pool", bufs=4))
@@ -39,10 +40,8 @@ def tile_moe_nxt_lin_relu_kernel(tc, xT, w_words, w_scales, b, wp, gate, offs, p
         w_t = [keep.tile([P, A, 2 * N], U8, name=f"w_t{e}", align_bytes=64) for e in range(E)]
         ws_t = keep.tile([P, E * A, N], U8, name="ws_t", align_bytes=64)
         b_t = keep.tile([P, R, E], F32, name="b_t")
-        gate_t = keep.tile([P, 2, T], F32, name="gate_t")
-        wp_raw = keep.tile([P, 4, M], F32, name="wp_raw")
 
-        nc.vector.memset(ws_t[:].rearrange("p g n -> p (g n)").bitcast(I32), 0)
+        nc.gpsimd.memset(ws_t[:].rearrange("p g n -> p (g n)").bitcast(I32), 0)
 
         nc.sync.dma_start(offs_t[:], offs)
         for a in range(A):
@@ -52,49 +51,44 @@ def tile_moe_nxt_lin_relu_kernel(tc, xT, w_words, w_scales, b, wp, gate, offs, p
         scale_rows = w_scales.rearrange("e a q n -> q (e a) n")
         for i in range(4):
             nc.sync.dma_start(out=ws_t[i:P:32, :, :].bitcast(I32), in_=scale_rows[i:16:4, :, :].bitcast(I32))
+        nc.sync.dma_start(out=b_t[:], in_=b.rearrange("(p r) e -> p r e", r=R))
         for e in range(E):
             nc.sync.dma_start(out=w_t[e][:].bitcast(I32), in_=w_words[e].rearrange("a p c -> p a c").bitcast(I32))
-            if e == 0:
-                nc.sync.dma_start(out=b_t[:], in_=b.rearrange("(p r) e -> p r e", r=R))
-        nc.sync.dma_start(pos1_t[:], pos1)
-        nc.sync.dma_start(pos2_t[:], pos2)
-        nc.sync.dma_start(out=gate_t[:], in_=gate[:, 0:P, :].rearrange("g p t -> p g t"))
-        nc.sync.dma_start(out=wp_raw[:], in_=wp.rearrange("(p j) f -> p j f", j=4))
 
         ident = keep.tile([P, P], F32, name="ident")
         make_identity(nc, ident[:])
 
-        codes = [keep.tile([P, T], U32, name=f"codes{a}", align_bytes=64) for a in range(A)]
-        planes = [keep.tile([P, T], U8, name=f"planes{a}", align_bytes=64) for a in range(A)]
-        slot_codes = [keep.tile([P, E * C], U32, name=f"slot_codes{a}", align_bytes=64) for a in range(A)]
-        slot_planes = [keep.tile([P, E * C], U8, name=f"slot_planes{a}", align_bytes=64) for a in range(A)]
+        codes = [keep.tile([P, WINDOW], I32, name=f"codes{a}", align_bytes=64) for a in range(A - 1)]
+        codes.append(late.tile([P, WINDOW], I32, name="codes2", tag="late1", align_bytes=64))
         for a in range(A):
-            nc.gpsimd.memset(planes[a][:].bitcast(I32), 0)
+            nc.vector.memset(codes[a][:, T:WINDOW], 0)
+        planes = late.tile([P, WINDOW], U8, name="planes", tag="late0", align_bytes=64)
+        packed = keep.tile([P, E * C], U8, name="packed", align_bytes=64)
+        slot_codes = [keep.tile([P, E * C], U32, name=f"slot_codes{a}", align_bytes=64) for a in range(A)]
+        slot_planes = [packed] + [keep.tile([P, E * C], U8, name=f"slot_planes{a}", align_bytes=64) for a in range(1, A)]
+        nc.gpsimd.memset(planes[:].bitcast(I32), 0)
+        for a in range(1, A):
+            nc.gpsimd.memset(slot_planes[a][:].bitcast(I32), 0)
 
         def quantise_pass(a):
+            x_b = keep.tile([P, T, 4], BF16, name=f"x_b{a}", align_bytes=64)
             for h in range(2):
-                cols = slice(h * HALF, (h + 1) * HALF)
-                x_b = keep.tile([P, HALF, 4], BF16, name=f"x_b{a}_{h}", align_bytes=64)
-                dst = x_b[:].rearrange("p (c i) j -> p c j i", i=4)
+                dst = x_b[:, h * HALF : (h + 1) * HALF, :].rearrange("p (c i) j -> p c j i", i=4)
                 src = x_raw[a][h][:].rearrange("p j (c i) -> p c j i", i=4)
-                if h == 0 and a != 1:
+                if a == 0:
                     nc.vector.tensor_copy(out=dst, in_=src)
                 else:
                     nc.scalar.activation(out=dst, in_=src, func=ACT.Copy)
-                nc.vector.quantize_mx(
-                    out=codes[a][:, cols].bitcast(FP8X4), scales=planes[a][:, cols], in_=x_b[:].rearrange("p c j -> p (c j)")
-                )
+            nc.vector.quantize_mx(
+                out=codes[a][:, 0:T].bitcast(FP8X4), scales=planes[4 * a : P, 0:T], in_=x_b[:].rearrange("p c j -> p (c j)")
+            )
 
-        def gather(a, chunk):
-            e0, e1 = chunk
-            slots = slice(e0 * C, e1 * C)
-            offsets = offs_t[:, e0 * C // 16 : e1 * C // 16]
-            nc.vector.tensor_copy(out=slot_codes[a][:, slots], in_=codes[a][:].indirect(offsets))
-            nc.vector.tensor_copy(out=slot_planes[a][:, slots], in_=planes[a][:].indirect(offsets))
+        def gather(out_tile, window):
+            nc.vector.tensor_copy(out=out_tile[:], in_=window.indirect(offs_t[:]))
 
         y = [keep.tile([P, E * C], F32, name=f"y{r}") for r in range(R)]
 
-        def expert(e):
+        def multiply(e):
             slots = slice(e * C, (e + 1) * C)
             acc = acc_pool.tile([P, N], F32)
             for a in range(A):
@@ -107,23 +101,43 @@ def tile_moe_nxt_lin_relu_kernel(tc, xT, w_words, w_scales, b, wp, gate, offs, p
                     start=(a == 0),
                     stop=(a == A - 1),
                 )
-            z = ring.tile([P, R, P], F32)
-            nc.scalar.activation(out=z[:], in_=acc[:].rearrange("s (m r) -> s r m", r=R), func=ACT.Copy)
-            turned = turn_pool.tile([P, R, C], F32)
-            for r in range(R):
-                nc.tensor.transpose(turned[:, r, :], z[:, r, :], ident[:])
-            for r in range(R):
-                nc.scalar.activation(out=y[r][:, slots], in_=turned[:, r, :], func=ACT.Relu, bias=b_t[:, r, e : e + 1], scale=1.0)
+            return acc
 
-        for a in range(A - 1):
+        def add_bias(e, acc):
+            z = ring.tile([P, R, P], F32)
+            nc.vector.tensor_tensor(z[:], acc[:].rearrange("s (m r) -> s r m", r=R), bias[e][:], ALU.add)
+            return z
+
+        for a in range(A):
             quantise_pass(a)
-            for chunk in CHUNKS:
-                gather(a, chunk)
-        quantise_pass(A - 1)
-        for chunk in CHUNKS:
-            gather(A - 1, chunk)
-            for e in range(chunk[0], chunk[1]):
-                expert(e)
+            if a < A - 1:
+                gather(slot_codes[a], codes[a][:].bitcast(U32))
+        gather(packed, planes[:])
+        for a in range(1, A):
+            for p0, p1 in ((0, 64), (64, 100)):
+                nc.sync.dma_start(out=slot_planes[a][p0:p1, :].bitcast(I32), in_=packed[p0 + 4 * a : p1 + 4 * a, :].bitcast(I32))
+        nc.sync.dma_start(pos1_t[:], pos1)
+        nc.sync.dma_start(pos2_t[:], pos2)
+        gate_t = late.tile([P, 2, T], F32, name="gate_t", tag="late0", align_bytes=64)
+        nc.sync.dma_start(out=gate_t[:], in_=gate[:, 0:P, :].rearrange("g p t -> p g t"))
+        wp_raw = late.tile([P, 4, M], F32, name="wp_raw", tag="late1", align_bytes=64)
+        nc.sync.dma_start(out=wp_raw[:], in_=wp.rearrange("(p j) f -> p j f", j=4))
+        gather(slot_codes[A - 1], codes[A - 1][:].bitcast(U32))
+        bias = [keep.tile([P, R, P], F32, name=f"bias{e}") for e in range(E)]
+        for e in range(E):
+            spread = turn_pool.tile([P, R, P], F32, name="spread", tag="turned")
+            for r in range(R):
+                nc.tensor.transpose(spread[:, r, :], b_t[:, r, e : e + 1].to_broadcast([P, P]), ident[:])
+            nc.scalar.activation(out=bias[e][:], in_=spread[:], func=ACT.Copy)
+
+        for g in range(2):
+            turned = [turn_pool.tile([P, 4, C], F32, name=f"turned{r}", tag="turned") for r in range(R)]
+            for e in range(4 * g, 4 * g + 4):
+                z = add_bias(e, multiply(e))
+                for r in range(R):
+                    nc.tensor.transpose(turned[r][:, e % 4, :], z[:, r, :], ident[:])
+            for r in range(R):
+                nc.scalar.activation(out=y[r][:, g * 4 * C : (g + 1) * 4 * C], in_=turned[r][:].rearrange("p e s -> p (e s)"), func=ACT.Relu)
 
         wp_b = keep.tile([P, M, 4], BF16, name="wp_b", align_bytes=64)
         nc.scalar.activation(
@@ -137,19 +151,23 @@ def tile_moe_nxt_lin_relu_kernel(tc, xT, w_words, w_scales, b, wp, gate, offs, p
             )
 
         out_rows = out.rearrange("(f p) t -> p f t", p=P)
+        g1 = keep.tile([P, R, T], F32, name="g1")
+        g2 = keep.tile([P, R, T], F32, name="g2")
+
+        def fetch(r, t0, t1):
+            for g, pos_t, k in ((g1, pos1_t, 0), (g2, pos2_t, 1)):
+                nc.vector.tensor_tensor(g[:, r, t0:t1], y[r][:].indirect(pos_t[:, t0 // 16 : t1 // 16]), gate_t[:, k, t0:t1], ALU.mult)
+
+        for r in range(R - 1):
+            fetch(r, 0, T)
         for h in range(2):
             toks = slice(h * HALF, (h + 1) * HALF)
-            idx = slice(h * HALF // 16, (h + 1) * HALF // 16)
-            g1 = keep.tile([P, R, HALF], F32, name=f"g1_{h}")
-            g2 = keep.tile([P, R, HALF], F32, name=f"g2_{h}")
-            for r in range(R):
-                nc.vector.tensor_tensor(g1[:, r, :], y[r][:].indirect(pos1_t[:, idx]), gate_t[:, 0, toks], ALU.mult)
-                nc.vector.tensor_tensor(g2[:, r, :], y[r][:].indirect(pos2_t[:, idx]), gate_t[:, 1, toks], ALU.mult)
+            fetch(R - 1, h * HALF, (h + 1) * HALF)
             c_b = keep.tile([P, HALF, R], BF16, name=f"c_b{h}", align_bytes=64)
             nc.vector.tensor_tensor(
                 c_b[:].rearrange("p (c i) r -> p c r i", i=4),
-                g1[:].rearrange("p r (c i) -> p c r i", i=4),
-                g2[:].rearrange("p r (c i) -> p c r i", i=4),
+                g1[:, :, toks].rearrange("p r (c i) -> p c r i", i=4),
+                g2[:, :, toks].rearrange("p r (c i) -> p c r i", i=4),
                 ALU.add,
             )
             c_codes = keep.tile([P, HALF], U32, name=f"c_codes{h}", align_bytes=64)

@@ -36,35 +36,38 @@ def tile_moe_nxt_lin_relu_kernel(tc, xT, w_words, w_scales, b, wp, gate, offs, p
         offs_t = keep.tile([P, E * C // 16], U16, name="offs_t")
         pos1_t = keep.tile([P, T // 16], U16, name="pos1_t")
         pos2_t = keep.tile([P, T // 16], U16, name="pos2_t")
-        x_raw = [[keep.tile([P, 4, HALF], F32, name=f"x_raw{a}_{h}") for h in range(2)] for a in range(A)]
-        w_t = [keep.tile([P, A, 2 * N], U8, name=f"w_t{e}", align_bytes=64) for e in range(E)]
+        x_raw = [keep.tile([P, 4, T], F32, name=f"x_raw{a}") for a in range(A)]
+        w_t = [keep.tile([P, 2 * A, 2 * N], U8, name=f"w_t{i}", align_bytes=64) for i in range(E // 2)]
         ws_t = keep.tile([P, E * A, N], U8, name="ws_t", align_bytes=64)
         b_t = keep.tile([P, R, E], F32, name="b_t")
 
-        nc.gpsimd.memset(ws_t[:].rearrange("p g n -> p (g n)").bitcast(I32), 0)
+        nc.vector.memset(ws_t[:].rearrange("p g n -> p (g n)").bitcast(I32), 0)
 
         nc.sync.dma_start(offs_t[:], offs)
         for a in range(A):
-            rows = xT[512 * a : 512 * (a + 1), :].rearrange("(p j) t -> p j t", j=4)
-            for h in range(2):
-                nc.sync.dma_start(out=x_raw[a][h][:], in_=rows[:, :, h * HALF : (h + 1) * HALF])
+            nc.sync.dma_start(out=x_raw[a][:], in_=xT[512 * a : 512 * (a + 1), :].rearrange("(p j) t -> p j t", j=4))
+        nc.sync.dma_start(out=b_t[:], in_=b.rearrange("(p r) e -> p r e", r=R))
         scale_rows = w_scales.rearrange("e a q n -> q (e a) n")
         for i in range(4):
             nc.sync.dma_start(out=ws_t[i:P:32, :, :].bitcast(I32), in_=scale_rows[i:16:4, :, :].bitcast(I32))
-        nc.sync.dma_start(out=b_t[:], in_=b.rearrange("(p r) e -> p r e", r=R))
-        for e in range(E):
-            nc.sync.dma_start(out=w_t[e][:].bitcast(I32), in_=w_words[e].rearrange("a p c -> p a c").bitcast(I32))
+        for i in range(E // 2):
+            nc.sync.dma_start(out=w_t[i][:].bitcast(I32), in_=w_words[2 * i : 2 * i + 2].rearrange("e a p c -> p (e a) c").bitcast(I32))
+
+        nc.sync.dma_start(pos1_t[:], pos1)
+        nc.sync.dma_start(pos2_t[:], pos2)
+        gate_t = keep.tile([P, 2, T], F32, name="gate_t")
+        nc.sync.dma_start(out=gate_t[:], in_=gate[:, 0:P, :].rearrange("g p t -> p g t"))
+        wp_raw = keep.tile([P, 4, M], F32, name="wp_raw")
+        nc.sync.dma_start(out=wp_raw[:], in_=wp.rearrange("(p j) f -> p j f", j=4))
 
         ident = keep.tile([P, P], F32, name="ident")
         make_identity(nc, ident[:])
 
-        codes = [keep.tile([P, WINDOW], I32, name=f"codes{a}", align_bytes=64) for a in range(A - 1)]
-        codes.append(late.tile([P, WINDOW], I32, name="codes2", tag="late1", align_bytes=64))
+        codes = [keep.tile([P, WINDOW], I32, name=f"codes{a}", align_bytes=64) for a in range(A)]
         for a in range(A):
             nc.vector.memset(codes[a][:, T:WINDOW], 0)
-        planes = late.tile([P, WINDOW], U8, name="planes", tag="late0", align_bytes=64)
+        planes = late.tile([P, WINDOW], U8, name="planes", tag="late", align_bytes=64)
         packed = keep.tile([P, E * C], U8, name="packed", align_bytes=64)
-        slot_codes = [keep.tile([P, E * C], U32, name=f"slot_codes{a}", align_bytes=64) for a in range(A)]
         slot_planes = [packed] + [keep.tile([P, E * C], U8, name=f"slot_planes{a}", align_bytes=64) for a in range(1, A)]
         nc.gpsimd.memset(planes[:].bitcast(I32), 0)
         for a in range(1, A):
@@ -74,8 +77,8 @@ def tile_moe_nxt_lin_relu_kernel(tc, xT, w_words, w_scales, b, wp, gate, offs, p
             x_b = keep.tile([P, T, 4], BF16, name=f"x_b{a}", align_bytes=64)
             for h in range(2):
                 dst = x_b[:, h * HALF : (h + 1) * HALF, :].rearrange("p (c i) j -> p c j i", i=4)
-                src = x_raw[a][h][:].rearrange("p j (c i) -> p c j i", i=4)
-                if a == 0:
+                src = x_raw[a][:, :, h * HALF : (h + 1) * HALF].rearrange("p j (c i) -> p c j i", i=4)
+                if a == 0 or h == 1:
                     nc.vector.tensor_copy(out=dst, in_=src)
                 else:
                     nc.scalar.activation(out=dst, in_=src, func=ACT.Copy)
@@ -83,8 +86,8 @@ def tile_moe_nxt_lin_relu_kernel(tc, xT, w_words, w_scales, b, wp, gate, offs, p
                 out=codes[a][:, 0:T].bitcast(FP8X4), scales=planes[4 * a : P, 0:T], in_=x_b[:].rearrange("p c j -> p (c j)")
             )
 
-        def gather(out_tile, window):
-            nc.vector.tensor_copy(out=out_tile[:], in_=window.indirect(offs_t[:]))
+        def gather(slots, window, e0, e1):
+            nc.vector.tensor_copy(out=slots[:, e0 * C : e1 * C], in_=window.indirect(offs_t[:, e0 * C // 16 : e1 * C // 16]))
 
         y = [keep.tile([P, E * C], F32, name=f"y{r}") for r in range(R)]
 
@@ -96,7 +99,7 @@ def tile_moe_nxt_lin_relu_kernel(tc, xT, w_words, w_scales, b, wp, gate, offs, p
                     out=acc[:],
                     lhsT=slot_codes[a][:, slots].bitcast(FP8X4),
                     lhsT_scale=slot_planes[a][:, slots],
-                    rhs=w_t[e][:, a, :].bitcast(FP4X4),
+                    rhs=w_t[e // 2][:, e % 2 * A + a, :].bitcast(FP4X4),
                     rhs_scale=ws_t[:, e * A + a, :],
                     start=(a == 0),
                     stop=(a == A - 1),
@@ -108,21 +111,20 @@ def tile_moe_nxt_lin_relu_kernel(tc, xT, w_words, w_scales, b, wp, gate, offs, p
             nc.vector.tensor_tensor(z[:], acc[:].rearrange("s (m r) -> s r m", r=R), bias[e][:], ALU.add)
             return z
 
-        for a in range(A):
-            quantise_pass(a)
-            if a < A - 1:
-                gather(slot_codes[a], codes[a][:].bitcast(U32))
-        gather(packed, planes[:])
+        slot_codes0 = keep.tile([P, E * C], U32, name="slot_codes0", align_bytes=64)
+        quantise_pass(0)
+        gather(slot_codes0[:], codes[0][:].bitcast(U32), 0, E)
+        quantise_pass(1)
+        quantise_pass(2)
+        gather(packed[:], planes[:], 0, E)
         for a in range(1, A):
             for p0, p1 in ((0, 64), (64, 100)):
-                nc.sync.dma_start(out=slot_planes[a][p0:p1, :].bitcast(I32), in_=packed[p0 + 4 * a : p1 + 4 * a, :].bitcast(I32))
-        nc.sync.dma_start(pos1_t[:], pos1)
-        nc.sync.dma_start(pos2_t[:], pos2)
-        gate_t = late.tile([P, 2, T], F32, name="gate_t", tag="late0", align_bytes=64)
-        nc.sync.dma_start(out=gate_t[:], in_=gate[:, 0:P, :].rearrange("g p t -> p g t"))
-        wp_raw = late.tile([P, 4, M], F32, name="wp_raw", tag="late1", align_bytes=64)
-        nc.sync.dma_start(out=wp_raw[:], in_=wp.rearrange("(p j) f -> p j f", j=4))
-        gather(slot_codes[A - 1], codes[A - 1][:].bitcast(U32))
+                nc.scalar.dma_start(out=slot_planes[a][p0:p1, :].bitcast(I32), in_=packed[p0 + 4 * a : p1 + 4 * a, :].bitcast(I32))
+        slot_codes12 = late.tile([P, 2, E * C], U32, name="slot_codes12", tag="late", align_bytes=64)
+        slot_codes = [slot_codes0[:], slot_codes12[:, 0, :], slot_codes12[:, 1, :]]
+        for e0 in (0, 4):
+            for a in range(1, A):
+                gather(slot_codes[a], codes[a][:].bitcast(U32), e0, e0 + 4)
         bias = [keep.tile([P, R, P], F32, name=f"bias{e}") for e in range(E)]
         for e in range(E):
             spread = turn_pool.tile([P, R, P], F32, name="spread", tag="turned")

from contextlib import ExitStack

import concourse.mybir as mybir
from concourse.masks import make_identity

K, T, E, C, N, M = 1536, 512, 8, 128, 512, 384
P = 128
A = 3
R = 4
HALF = 256
WINDOW = 1376
FLOPS = 2 * K * N * E * C + 2 * N * M * T
BYTES = 4 * K * T + E * K * N // 2 + E * K * N // 32 + 4 * N * E + 4 * N * M + 4 * 2 * T + 2 * 128 * 128 + 4 * M * T

F32 = mybir.dt.float32
BF16 = mybir.dt.bfloat16
I32 = mybir.dt.int32
U32 = mybir.dt.uint32
U16 = mybir.dt.uint16
U8 = mybir.dt.uint8
FP8X4 = mybir.dt.float8_e4m3fn_x4
FP4X4 = mybir.dt.float4_e2m1fn_x4
ACT = mybir.ActivationFunctionType
ALU = mybir.AluOpType


def tile_moe_nxt_lin_relu_kernel(tc, xT, w_words, w_scales, b, wp, gate, offs, pos1, pos2, out):
    nc = tc.nc
    with ExitStack() as ctx:
        keep = ctx.enter_context(tc.tile_pool(name="keep", bufs=1))
        late = ctx.enter_context(tc.tile_pool(name="late", bufs=1))
        ring = ctx.enter_context(tc.tile_pool(name="ring", bufs=3))
        acc_pool = ctx.enter_context(tc.psum_pool(name="acc_pool", bufs=4))
        turn_pool = ctx.enter_context(tc.psum_pool(name="turn_pool", bufs=4))

        offs_t = keep.tile([P, E * C // 16], U16, name="offs_t")
        pos1_t = keep.tile([P, T // 16], U16, name="pos1_t")
        pos2_t = keep.tile([P, T // 16], U16, name="pos2_t")
        x_raw = [keep.tile([P, 4, T], F32, name=f"x_raw{a}") for a in range(A)]
        w_t = [keep.tile([P, 2 * A, 2 * N], U8, name=f"w_t{i}", align_bytes=64) for i in range(E // 2)]
        ws_t = keep.tile([P, E * A, N], U8, name="ws_t", align_bytes=64)
        b_t = keep.tile([P, R, E], F32, name="b_t")

        nc.vector.memset(ws_t[:].rearrange("p g n -> p (g n)").bitcast(I32), 0)

        nc.sync.dma_start(offs_t[:], offs)
        for a in range(A):
            nc.sync.dma_start(out=x_raw[a][:], in_=xT[512 * a : 512 * (a + 1), :].rearrange("(p j) t -> p j t", j=4))
        nc.sync.dma_start(out=b_t[:], in_=b.rearrange("(p r) e -> p r e", r=R))
        scale_rows = w_scales.rearrange("e a q n -> q (e a) n")
        for i in range(4):
            nc.sync.dma_start(out=ws_t[i:P:32, :, :].bitcast(I32), in_=scale_rows[i:16:4, :, :].bitcast(I32))
        for i in range(E // 2):
            nc.sync.dma_start(out=w_t[i][:].bitcast(I32), in_=w_words[2 * i : 2 * i + 2].rearrange("e a p c -> p (e a) c").bitcast(I32))

        nc.sync.dma_start(pos1_t[:], pos1)
        nc.sync.dma_start(pos2_t[:], pos2)
        gate_t = keep.tile([P, 2, T], F32, name="gate_t")
        nc.sync.dma_start(out=gate_t[:], in_=gate[:, 0:P, :].rearrange("g p t -> p g t"))
        wp_raw = keep.tile([P, 4, M], F32, name="wp_raw")
        nc.sync.dma_start(out=wp_raw[:], in_=wp.rearrange("(p j) f -> p j f", j=4))

        ident = keep.tile([P, P], F32, name="ident")
        make_identity(nc, ident[:])

        codes = [keep.tile([P, WINDOW], I32, name=f"codes{a}", align_bytes=64) for a in range(A)]
        for a in range(A):
            nc.vector.memset(codes[a][:, T:WINDOW], 0)
        planes = late.tile([P, WINDOW], U8, name="planes", tag="late", align_bytes=64)
        packed = keep.tile([P, E * C], U8, name="packed", align_bytes=64)
        slot_planes = [packed] + [keep.tile([P, E * C], U8, name=f"slot_planes{a}", align_bytes=64) for a in range(1, A)]
        nc.gpsimd.memset(planes[:].bitcast(I32), 0)
        for a in range(1, A):
            nc.gpsimd.memset(slot_planes[a][:].bitcast(I32), 0)

        def quantise_pass(a):
            x_b = keep.tile([P, T, 4], BF16, name=f"x_b{a}", align_bytes=64)
            for h in range(2):
                dst = x_b[:, h * HALF : (h + 1) * HALF, :].rearrange("p (c i) j -> p c j i", i=4)
                src = x_raw[a][:, :, h * HALF : (h + 1) * HALF].rearrange("p j (c i) -> p c j i", i=4)
                if a == 0 or h == 1:
                    nc.vector.tensor_copy(out=dst, in_=src)
                else:
                    nc.scalar.activation(out=dst, in_=src, func=ACT.Copy)
            nc.vector.quantize_mx(
                out=codes[a][:, 0:T].bitcast(FP8X4), scales=planes[4 * a : P, 0:T], in_=x_b[:].rearrange("p c j -> p (c j)")
            )

        def gather(slots, window, e0, e1):
            nc.vector.tensor_copy(out=slots[:, e0 * C : e1 * C], in_=window.indirect(offs_t[:, e0 * C // 16 : e1 * C // 16]))

        y = [keep.tile([P, E * C], F32, name=f"y{r}") for r in range(R)]

        def multiply(e):
            slots = slice(e * C, (e + 1) * C)
            acc = acc_pool.tile([P, N], F32)
            for a in range(A):
                nc.tensor.matmul_mx(
                    out=acc[:],
                    lhsT=slot_codes[a][:, slots].bitcast(FP8X4),
                    lhsT_scale=slot_planes[a][:, slots],
                    rhs=w_t[e // 2][:, e % 2 * A + a, :].bitcast(FP4X4),
                    rhs_scale=ws_t[:, e * A + a, :],
                    start=(a == 0),
                    stop=(a == A - 1),
                )
            return acc

        def add_bias(e, acc):
            z = ring.tile([P, R, P], F32)
            nc.vector.tensor_tensor(z[:], acc[:].rearrange("s (m r) -> s r m", r=R), bias[e][:], ALU.add)
            return z

        slot_codes0 = keep.tile([P, E * C], U32, name="slot_codes0", align_bytes=64)
        quantise_pass(0)
        gather(slot_codes0[:], codes[0][:].bitcast(U32), 0, E)
        quantise_pass(1)
        quantise_pass(2)
        gather(packed[:], planes[:], 0, E)
        for a in range(1, A):
            for p0, p1 in ((0, 64), (64, 100)):
                nc.scalar.dma_start(out=slot_planes[a][p0:p1, :].bitcast(I32), in_=packed[p0 + 4 * a : p1 + 4 * a, :].bitcast(I32))
        slot_codes12 = late.tile([P, 2, E * C], U32, name="slot_codes12", tag="late", align_bytes=64)
        slot_codes = [slot_codes0[:], slot_codes12[:, 0, :], slot_codes12[:, 1, :]]
        for e0 in (0, 4):
            for a in range(1, A):
                gather(slot_codes[a], codes[a][:].bitcast(U32), e0, e0 + 4)
        bias = [keep.tile([P, R, P], F32, name=f"bias{e}") for e in range(E)]
        for e in range(E):
            spread = turn_pool.tile([P, R, P], F32, name="spread", tag="turned")
            for r in range(R):
                nc.tensor.transpose(spread[:, r, :], b_t[:, r, e : e + 1].to_broadcast([P, P]), ident[:])
            nc.scalar.activation(out=bias[e][:], in_=spread[:], func=ACT.Copy)

        for g in range(2):
            turned = [turn_pool.tile([P, 4, C], F32, name=f"turned{r}", tag="turned") for r in range(R)]
            for e in range(4 * g, 4 * g + 4):
                z = add_bias(e, multiply(e))
                for r in range(R):
                    nc.tensor.transpose(turned[r][:, e % 4, :], z[:, r, :], ident[:])
            for r in range(R):
                nc.scalar.activation(out=y[r][:, g * 4 * C : (g + 1) * 4 * C], in_=turned[r][:].rearrange("p e s -> p (e s)"), func=ACT.Relu)

        wp_b = keep.tile([P, M, 4], BF16, name="wp_b", align_bytes=64)
        nc.scalar.activation(
            out=wp_b[:].rearrange("p (c i) j -> p c j i", i=4), in_=wp_raw[:].rearrange("p j (c i) -> p c j i", i=4), func=ACT.Copy
        )
        wp_codes = keep.tile([P, M], U32, name="wp_codes", align_bytes=64)
        wp_planes = keep.tile([P, M], U8, name="wp_planes", align_bytes=64)
        for lo, hi in ((0, 256), (256, 384)):
            nc.vector.quantize_mx(
                out=wp_codes[:, lo:hi].bitcast(FP8X4), scales=wp_planes[:, lo:hi], in_=wp_b[:, lo:hi, :].rearrange("p c j -> p (c j)")
            )

        out_rows = out.rearrange("(f p) t -> p f t", p=P)
        g1 = keep.tile([P, R, T], F32, name="g1")
        g2 = keep.tile([P, R, T], F32, name="g2")

        def fetch(r, t0, t1):
            for g, pos_t, k in ((g1, pos1_t, 0), (g2, pos2_t, 1)):
                nc.vector.tensor_tensor(g[:, r, t0:t1], y[r][:].indirect(pos_t[:, t0 // 16 : t1 // 16]), gate_t[:, k, t0:t1], ALU.mult)

        for r in range(R - 1):
            fetch(r, 0, T)
        for h in range(2):
            toks = slice(h * HALF, (h + 1) * HALF)
            fetch(R - 1, h * HALF, (h + 1) * HALF)
            c_b = keep.tile([P, HALF, R], BF16, name=f"c_b{h}", align_bytes=64)
            nc.vector.tensor_tensor(
                c_b[:].rearrange("p (c i) r -> p c r i", i=4),
                g1[:, :, toks].rearrange("p r (c i) -> p c r i", i=4),
                g2[:, :, toks].rearrange("p r (c i) -> p c r i", i=4),
                ALU.add,
            )
            c_codes = keep.tile([P, HALF], U32, name=f"c_codes{h}", align_bytes=64)
            c_planes = keep.tile([P, HALF], U8, name=f"c_planes{h}", align_bytes=64)
            nc.vector.quantize_mx(out=c_codes[:].bitcast(FP8X4), scales=c_planes[:], in_=c_b[:].rearrange("p c r -> p (c r)"))
            result = keep.tile([P, 3, HALF], F32, name=f"result{h}")
            for f0, f1 in ((0, 2), (2, 3)):
                acc = acc_pool.tile([P, N], F32)
                for f in range(f0, f1):
                    nc.tensor.matmul_mx(
                        out=acc[:, (f - f0) * HALF : (f - f0 + 1) * HALF],
                        lhsT=wp_codes[:, f * P : (f + 1) * P].bitcast(FP8X4),
                        lhsT_scale=wp_planes[:, f * P : (f + 1) * P],
                        rhs=c_codes[:].bitcast(FP8X4),
                        rhs_scale=c_planes[:],
                        start=True,
                        stop=True,
                    )
                sums = acc[:, 0 : (f1 - f0) * HALF].rearrange("p (f t) -> p f t", t=HALF)
                if h == 1 and f0 == 2:
                    nc.vector.tensor_copy(out=result[:, f0:f1, :], in_=sums)
                else:
                    nc.scalar.activation(out=result[:, f0:f1, :], in_=sums, func=ACT.Copy)
                nc.sync.dma_start(out=out_rows[:, f0:f1, toks], in_=result[:, f0:f1, :])
